import numpy as np
import ml_dtypes


def mxq(x, axis, fmt="e4m3"):
    dtype, down = {"e4m3": (ml_dtypes.float8_e4m3fn, 7), "e5m2": (ml_dtypes.float8_e5m2, 14)}[fmt]
    v = np.moveaxis(np.asarray(x, np.float32).astype(ml_dtypes.bfloat16).astype(np.float64), axis, -1)
    blocks = v.reshape(v.shape[:-1] + (-1, 32))
    amax = np.abs(blocks).max(-1, keepdims=True)
    byte = np.maximum(np.where(amax > 0, np.frexp(amax)[1] - 1 + 127, 0) - down, 1)
    scale = np.exp2(byte - 127.0)
    codes = (blocks / scale).astype(np.float32).astype(dtype).astype(np.float64)
    return np.moveaxis((codes * scale).reshape(v.shape), -1, axis)


WIDE = False


def mx_kscale(k):
    if not WIDE:
        return np.ones(k)
    levels = np.array([10, -10, 5, -5, 0])
    if k % 512:
        return np.exp2(np.random.permutation(np.resize(levels, k // 32))).repeat(32)
    a = np.empty((k // 512, 16))
    for p in range(k // 512):
        a[p, :8] = np.random.permutation(np.resize(levels, 8))
        for g in range(8):
            far = levels[np.abs(levels - a[p, g]) >= 10]
            a[p, g + 8] = far[np.random.randint(len(far))]
    return np.exp2(a.ravel()).repeat(32)


def f64(x):
    return np.asarray(x).astype(np.float64)


def striped(idx):
    return np.tile(idx.reshape(-1, 16).T, (8, 1)).astype(np.uint16)


def unstriped(offs):
    return offs[:16].T.reshape(-1).astype(np.int64)


def striped8(idx):
    return np.concatenate([x.reshape(-1, 16).T for x in idx]).astype(np.uint16)


def runs(offs, k):
    lists = np.stack([offs[16 * r : 16 * r + 16].T.reshape(-1) for r in range(8)]).astype(np.int64)
    return lists[np.arange(k) % 512 // 64]


def pack_weight(w):
    k, n = w.shape
    w = f64(np.asarray(w, np.float32).astype(ml_dtypes.bfloat16)).reshape(k // 32, 32, n)
    amax = np.abs(w).max(1)
    byte = np.clip(np.where(amax > 0, np.frexp(amax)[1] - 1 + 127 - 7, 1), 1, 254)
    scaled = (w * np.exp2(127.0 - byte)[:, None, :]).reshape(k, n).astype(np.float32)
    words = np.ascontiguousarray(scaled.reshape(k // 512, 128, 4, n).transpose(0, 1, 3, 2)).astype(ml_dtypes.float8_e4m3fn).view(np.uint8)
    return words, np.ascontiguousarray(byte.astype(np.uint8).reshape(k // 512, 16, n))


def unpack_weight(words, scales):
    g, p, n, _ = words.shape
    vals = np.ascontiguousarray(words).view(ml_dtypes.float8_e4m3fn).astype(np.float64) * np.repeat(np.exp2(scales.astype(np.float64) - 127.0), 8, axis=1)[..., None]
    return vals.transpose(0, 1, 3, 2).reshape(g * 512, n)


K, T, S, N, H, W = 512, 2048, 512, 512, 512, 2048


def setup_inputs():
    n = np.random.standard_normal
    s = mx_kscale(K)[:, None]
    u = mx_kscale(H)
    packed_xT = pack_weight(n((K, T)) * s)
    return {
        "x_words": packed_xT[0],
        "x_scales": packed_xT[1],
        "w1": (n((K, H)) / np.sqrt(K) / s).astype(np.float32),
        "gn": (np.random.uniform(0.5, 1.5, (H, 1)) * u[:, None]).astype(np.float32),
        "w2": (n((H, N)) / np.sqrt(2 * H) / u[:, None]).astype(np.float32),
        "w3": (n((K, N)) / np.sqrt(2 * K) / s).astype(np.float32),
        "tau": np.random.uniform(0.3, 0.9, (N, 1)).astype(np.float32),
        "offs": striped(np.random.permutation(T)[:S]),
        "n1": striped(np.random.permutation(S)),
        "n2": striped(np.random.permutation(S)),
        "n3": striped(np.random.permutation(S)),
        "hz": striped8(np.random.randint(0, T, (8, S))),
        "n4": striped(np.random.randint(0, S, W)),
    }


def reference(x_words, x_scales, w1, gn, w2, w3, tau, offs, n1, n2, n3, hz, n4):
    xq = unpack_weight(x_words, x_scales)[:, unstriped(offs)]
    y = mxq(f64(w1), 0, "e4m3").T @ xq
    ex = np.exp(0.5 * y)
    z = f64(gn) * (np.log((ex + ex[:, unstriped(n1)]) / (ex[:, unstriped(n2)] + ex[:, unstriped(n3)])))
    x_hz = unpack_weight(x_words, x_scales)[np.arange(K)[:, None], runs(hz, K)]
    h = mxq(f64(w2), 0, "e4m3").T @ mxq(z, 0, "e4m3") + mxq(f64(w3), 0, "e4m3").T @ x_hz
    top = h.max(axis=1, keepdims=True)
    ea = np.exp(f64(tau) * (h[:, unstriped(n4)] - top))
    ms = ea.reshape(N, S, 4).sum(axis=2)
    return np.log(ms + 0.25) - (0.5 * h)

@@ -1,0 +1,260 @@
+from contextlib import ExitStack
+
+import concourse.mybir as mybir
+
+K, T, S, N, H, W = 512, 2048, 512, 512, 512, 2048
+FLOPS = 3 * 2 * 512 * 512 * 512
+
+F32 = mybir.dt.float32
+BF16 = mybir.dt.bfloat16
+I32 = mybir.dt.int32
+U32 = mybir.dt.uint32
+U16 = mybir.dt.uint16
+U8 = mybir.dt.uint8
+FP8X4 = mybir.dt.float8_e4m3fn_x4
+ACT = mybir.ActivationFunctionType
+ALU = mybir.AluOpType
+AX = mybir.AxisListType
+
+P = 128
+PACK = 4
+LANES = 16
+CHUNK = 128
+HALF = 256
+PIECE = 512
+MEMBERS = 4
+
+
+def tile_picked_mixhoddsegl_none_p_kernel(
+    tc, x_words, x_scales, w1, gn, w2, w3, tau, offs, n1, n2, n3, hz, n4, out
+):
+    nc = tc.nc
+
+    def entries(list_tile, a, b):
+        return list_tile[:, a // LANES : b // LANES]
+
+    def mx(dst, lhs_codes, lhs_scales, rhs_codes, rhs_scales, start, stop):
+        nc.tensor.matmul_mx(
+            out=dst,
+            lhsT=lhs_codes.bitcast(FP8X4),
+            lhsT_scale=lhs_scales,
+            rhs=rhs_codes.bitcast(FP8X4),
+            rhs_scale=rhs_scales,
+            start=start,
+            stop=stop,
+        )
+
+    with ExitStack() as ctx:
+        keep = ctx.enter_context(tc.tile_pool(name="keep", bufs=1))
+        ring = ctx.enter_context(tc.tile_pool(name="ring", bufs=4))
+        pair_ring = ctx.enter_context(tc.tile_pool(name="pair_ring", bufs=2))
+        psum = ctx.enter_context(tc.psum_pool(name="psum", bufs=1))
+
+        def held(name, shape, dtype):
+            return keep.tile(shape, dtype, name=name, align_bytes=64)
+
+        offs_t = held("offs_t", [P, S // LANES], U16)
+        n1_t = held("n1_t", [P, S // LANES], U16)
+        n2_t = held("n2_t", [P, S // LANES], U16)
+        n3_t = held("n3_t", [P, S // LANES], U16)
+        hz_t = held("hz_t", [P, S // LANES], U16)
+        n4_t = held("n4_t", [P, W // LANES], U16)
+
+        xw = held("xw", [P, T], U32)
+        xs = held("xs", [P, T], U8)
+        hs = held("hs", [P, T], U8)
+        w1_raw = held("w1_raw", [P, PACK, H], F32)
+        w23_raw = held("w23_raw", [P, 2, PACK, N], F32)
+        gn_t = held("gn_t", [P, PACK], F32)
+        tau_t = held("tau_t", [P, PACK], F32)
+        hz_scales = held("hz_scales", [P, S], U8)
+        h_t = [held("h%d" % m, [P, (4 if m == 3 else 2) * S], F32) for m in range(4)]
+
+        scale_rows = x_scales[0].bitcast(I32)
+
+        nc.vector.memset(xs[:].bitcast(I32), 0)
+        nc.vector.memset(hs[:].bitcast(I32), 0)
+        nc.vector.memset(hz_scales[:].bitcast(I32), 0)
+        for m in range(4):
+            nc.vector.memset(h_t[m][:, S:], 0.0)
+
+        nc.sync.dma_start(w1_raw[:], w1.rearrange("(p j) c -> p j c", j=PACK))
+        for q in range(4):
+            nc.sync.dma_start(xs[32 * q : 32 * q + 4, :].bitcast(I32), scale_rows[4 * q : 4 * q + 4, :])
+        nc.sync.dma_start(offs_t[:], offs)
+        nc.sync.dma_start(xw[:].bitcast(I32), x_words[0].rearrange("p n t -> p (n t)").bitcast(I32))
+        nc.sync.dma_start(hz_t[:], hz)
+        for e in range(2):
+            nc.sync.dma_start(hs[e:P:LANES, :].bitcast(I32), scale_rows[e:16:2, :])
+        nc.sync.dma_start(n3_t[:], n3)
+        nc.sync.dma_start(n1_t[:], n1)
+        nc.sync.dma_start(n2_t[:], n2)
+        nc.sync.dma_start(gn_t[:], gn.rearrange("(p t) o -> p (t o)", t=PACK))
+        nc.sync.dma_start(w23_raw[:, 0], w2.rearrange("(p j) c -> p j c", j=PACK))
+        nc.sync.dma_start(w23_raw[:, 1], w3.rearrange("(p j) c -> p j c", j=PACK))
+        nc.sync.dma_start(n4_t[:], n4)
+        with nc.allow_non_contiguous_dma(reason="one rate for each partition and row tile"):
+            nc.sync.dma_start(tau_t[:], tau.rearrange("(m p) o -> p (m o)", p=P))
+
+        w1_bf = held("w1_bf", [P, PACK, P, PACK], BF16)
+        w1_dst = w1_bf[:].rearrange("p t m j -> p m j t")
+        w1_src = w1_raw[:].rearrange("p j (m t) -> p m j t", t=PACK)
+        nc.scalar.activation(w1_dst[:, : P // 2], w1_src[:, : P // 2], ACT.Copy)
+        nc.vector.tensor_copy(w1_dst[:, P // 2 :], w1_src[:, P // 2 :])
+        x_bytes = held("x_bytes", [P, S], U8)
+        nc.vector.tensor_copy(x_bytes[:], xs[:].indirect(offs_t[:]))
+        w1_codes = held("w1_codes", [P, H], U32)
+        w1_scales = held("w1_scales", [P, H], U8)
+        nc.vector.quantize_mx(
+            out=w1_codes[:].bitcast(FP8X4), scales=w1_scales[:], in_=w1_bf[:].rearrange("p t m j -> p (t m j)")
+        )
+        x_codes = held("x_codes", [P, S], U32)
+
+        ex = held("ex", [P, PACK, S], F32)
+        for a in range(0, S, HALF):
+            cols = slice(a, a + HALF)
+            nc.vector.tensor_copy(x_codes[:, cols], xw[:].indirect(entries(offs_t, a, a + HALF)))
+            for pair in range(2):
+                y_bank = psum.tile([P, 2, HALF], F32, name="y%d_%d" % (a, pair))
+                for u in range(2):
+                    rows = slice((2 * pair + u) * P, (2 * pair + u + 1) * P)
+                    mx(y_bank[:, u, :], w1_codes[:, rows], w1_scales[:, rows], x_codes[:, cols], x_bytes[:, cols], True, True)
+                nc.scalar.activation(ex[:, 2 * pair : 2 * pair + 2, cols], y_bank[:], ACT.Exp, scale=0.5)
+
+        hz_codes = held("hz_codes", [P, S], U32)
+        hz_bytes = held("hz_bytes", [P, S], U8)
+        nc.vector.tensor_copy(hz_codes[:], xw[:].indirect(hz_t[:]))
+        nc.vector.tensor_copy(hz_bytes[:], hs[:].indirect(hz_t[:]))
+        for odd in range(2):
+            for e in range(2):
+                nc.sync.dma_start(
+                    hz_scales[2 * odd + e : P : 32, :].bitcast(I32), hz_bytes[LANES * odd + e : P : 32, :].bitcast(I32)
+                )
+
+        ex_n2 = held("ex_n2", [P, PACK, S], F32)
+        for t in range(PACK):
+            for a in range(0, S, HALF):
+                nc.vector.tensor_copy(ex_n2[:, t, a : a + HALF], ex[:, t, :].indirect(entries(n2_t, a, a + HALF)))
+
+        w23_codes = [held("w23_codes%d" % m, [P, 2 * P], U32) for m in range(4)]
+        w23_scales = [held("w23_scales%d" % m, [P, 2 * P], U8) for m in range(4)]
+
+        def stage(name, shape, dtype):
+            return keep.tile(shape, dtype, name=name, tag="stage", align_bytes=64)
+
+        def quantize_w23(m):
+            bf = stage("w23_bf", [P, 2, P, PACK], BF16)
+            nc.vector.tensor_copy(
+                bf[:].rearrange("p w (c i) j -> p w c j i", i=4),
+                w23_raw[:, :, :, m * P : (m + 1) * P].rearrange("p w j (c i) -> p w c j i", i=4),
+            )
+            nc.vector.quantize_mx(
+                out=w23_codes[m][:].bitcast(FP8X4),
+                scales=w23_scales[m][:],
+                in_=bf[:].rearrange("p w c j -> p (w c j)"),
+            )
+
+        z_codes = held("z_codes", [P, S], U32)
+        z_scales = held("z_scales", [P, S], U8)
+        h_bank = [psum.tile([P, S], F32, name="hb%d" % m) for m in range(4)]
+        h_end = psum.tile([P, CHUNK], F32, name="h_end", tag="y0_0")
+        bias = held("bias", [P, 4], F32)
+        sums = {}
+
+        def look_up(a):
+            b = a + CHUNK
+            ab = pair_ring.tile([P, 2, PACK, CHUNK], F32, name="ab")
+            ex_n3 = pair_ring.tile([P, PACK, CHUNK], F32, name="ex_n3")
+            for t in range(PACK):
+                nc.scalar.activation(ex_n3[:, t, :], ex[:, t, :].indirect(entries(n3_t, a, b)), ACT.Copy)
+            for t in range(PACK):
+                nc.scalar.activation(ab[:, 0, t, :], ex[:, t, :].indirect(entries(n1_t, a, b)), ACT.Copy)
+            nc.vector.tensor_tensor(ab[:, 1], ex_n2[:, :, a:b], ex_n3[:], ALU.add)
+            nc.vector.tensor_tensor(ab[:, 0], ab[:, 0], ex[:, :, a:b], ALU.add)
+            sums[a] = ab
+
+        def make_z(a, parts):
+            b = a + CHUNK
+            ab = sums[a]
+            logs = pair_ring.tile([P, 2, PACK, CHUNK], F32, name="logs")
+            diff = pair_ring.tile([P, PACK, CHUNK], F32, name="diff")
+            z_bf = pair_ring.tile([P, CHUNK, PACK], BF16, name="z_bf", align_bytes=64)
+            step = CHUNK // parts
+            for c in range(0, CHUNK, step):
+                cols = slice(c, c + step)
+                nc.scalar.activation(logs[:, :, :, cols], ab[:, :, :, cols], ACT.Ln)
+                nc.vector.tensor_tensor(diff[:, :, cols], logs[:, 0, :, cols], logs[:, 1, :, cols], ALU.subtract)
+                nc.vector.tensor_tensor(
+                    z_bf[:, cols, :].rearrange("p (c i) t -> p c t i", i=4),
+                    diff[:, :, cols].rearrange("p t (c i) -> p c t i", i=4),
+                    gn_t[:].unsqueeze(1).unsqueeze(3).to_broadcast([P, step // 4, PACK, 4]),
+                    ALU.mult,
+                )
+            nc.vector.quantize_mx(
+                out=z_codes[:, a:b].bitcast(FP8X4), scales=z_scales[:, a:b], in_=z_bf[:].rearrange("p n t -> p (n t)")
+            )
+
+        def product(dst, m, a, b):
+            mx(dst, w23_codes[m][:, P:], w23_scales[m][:, P:], hz_codes[:, a:b], hz_scales[:, a:b], True, False)
+            mx(dst, w23_codes[m][:, :P], w23_scales[m][:, :P], z_codes[:, a:b], z_scales[:, a:b], False, True)
+
+        def evacuate(dst, src, so_far, top):
+            nc.vector.tensor_scalar(dst, src, 1.0, so_far, ALU.mult, ALU.max, accum_out=top)
+
+        def make_bias(m, top):
+            nc.vector.tensor_scalar(bias[:, m : m + 1], top, tau_t[:, m : m + 1], -1.0, ALU.mult, ALU.mult)
+
+        last = S - CHUNK
+        look_up(0)
+        quantize_w23(0)
+        for a in range(0, last, CHUNK):
+            look_up(a + CHUNK)
+            make_z(a, 1)
+            product(h_bank[0][:, a : a + CHUNK], 0, a, a + CHUNK)
+        tops = stage("tops", [P, 2], F32)
+        evacuate(h_t[0][:, :last], h_bank[0][:, :last], None, tops[:, 0:1])
+        make_z(last, 2)
+        product(h_end[:], 0, last, S)
+        evacuate(h_t[0][:, last:S], h_end[:], tops[:, 0:1], tops[:, 1:2])
+        make_bias(0, tops[:, 1:2])
+
+        ms = held("ms", [P, 4, S], F32)
+
+        def members(m):
+            for a in range(0, W, PIECE):
+                ea = ring.tile([P, PIECE], F32, name="ea")
+                nc.scalar.activation(
+                    ea[:],
+                    h_t[m][:].indirect(entries(n4_t, a, a + PIECE)),
+                    ACT.Exp,
+                    bias=bias[:, m : m + 1],
+                    scale=tau_t[:, m : m + 1],
+                )
+                nc.vector.tensor_reduce(
+                    ms[:, m, a // MEMBERS : (a + PIECE) // MEMBERS],
+                    ea[:].rearrange("p (j t) -> p j t", t=MEMBERS),
+                    AX.X,
+                    ALU.add,
+                )
+
+        for m in range(4):
+            if m + 1 < 4:
+                quantize_w23(m + 1)
+                product(h_bank[m + 1][:], m + 1, 0, S)
+                top = stage("top", [P, 1], F32)
+                evacuate(h_t[m + 1][:, :S], h_bank[m + 1][:], None, top[:])
+                make_bias(m + 1, top[:])
+            members(m)
+
+        last_log = held("last_log", [P, S], F32)
+        result = held("result", [P, 4, S], F32)
+        for m in range(4):
+            log_ms = last_log[:] if m == 3 else h_t[3][:, (m + 1) * S : (m + 2) * S]
+            step = S // 2 if m == 3 else S
+            for a in range(0, S, step):
+                cols = slice(a, a + step)
+                nc.scalar.activation(log_ms[:, cols], ms[:, m, cols], ACT.Ln, bias=0.25)
+                nc.vector.scalar_tensor_tensor(
+                    result[:, m, cols], h_t[m][:, cols], -0.5, log_ms[:, cols], ALU.mult, ALU.add
+                )
+                nc.sync.dma_start(out[m * P : (m + 1) * P, cols], result[:, m, cols])

@@ -20,8 +20,9 @@ P = 128
 PACK = 4
 LANES = 16
 CHUNK = 128
-HALF = 256
-PIECE = 512
+PIECE = 1024
+FIRST = 320
+SHORT = 64
 MEMBERS = 4
 
 
@@ -46,8 +47,7 @@ def tile_picked_mixhoddsegl_none_p_kernel(
 
     with ExitStack() as ctx:
         keep = ctx.enter_context(tc.tile_pool(name="keep", bufs=1))
-        ring = ctx.enter_context(tc.tile_pool(name="ring", bufs=4))
-        pair_ring = ctx.enter_context(tc.tile_pool(name="pair_ring", bufs=2))
+        ring = ctx.enter_context(tc.tile_pool(name="ring", bufs=6))
         psum = ctx.enter_context(tc.psum_pool(name="psum", bufs=1))
 
         def held(name, shape, dtype):
@@ -63,22 +63,25 @@ def tile_picked_mixhoddsegl_none_p_kernel(
         xw = held("xw", [P, T], U32)
         xs = held("xs", [P, T], U8)
         hs = held("hs", [P, T], U8)
-        w1_raw = held("w1_raw", [P, PACK, H], F32)
-        w23_raw = held("w23_raw", [P, 2, PACK, N], F32)
         gn_t = held("gn_t", [P, PACK], F32)
         tau_t = held("tau_t", [P, PACK], F32)
         hz_scales = held("hz_scales", [P, S], U8)
-        h_t = [held("h%d" % m, [P, (4 if m == 3 else 2) * S], F32) for m in range(4)]
+        h_t = [held("h%d" % m, [P, (1 + PACK) * S], F32) for m in range(4)]
+        ex_n2, w1_raw, w2_raw, w3_raw = [h[:, S:].rearrange("p (j c) -> p j c", j=PACK) for h in h_t]
+        ex = held("ex", [P, PACK + 1, S], F32)
+        ex_row = ex[:].rearrange("p t s -> p (t s)")
+
+        def ex_window(t):
+            return ex_row[:, t * S : (t + 2) * S]
 
         scale_rows = x_scales[0].bitcast(I32)
 
         nc.vector.memset(xs[:].bitcast(I32), 0)
         nc.vector.memset(hs[:].bitcast(I32), 0)
         nc.vector.memset(hz_scales[:].bitcast(I32), 0)
-        for m in range(4):
-            nc.vector.memset(h_t[m][:, S:], 0.0)
+        nc.vector.memset(ex[:, PACK, :], 0.0)
 
-        nc.sync.dma_start(w1_raw[:], w1.rearrange("(p j) c -> p j c", j=PACK))
+        nc.sync.dma_start(w1_raw, w1.rearrange("(p j) c -> p j c", j=PACK))
         for q in range(4):
             nc.sync.dma_start(xs[32 * q : 32 * q + 4, :].bitcast(I32), scale_rows[4 * q : 4 * q + 4, :])
         nc.sync.dma_start(offs_t[:], offs)
@@ -90,15 +93,15 @@ def tile_picked_mixhoddsegl_none_p_kernel(
         nc.sync.dma_start(n1_t[:], n1)
         nc.sync.dma_start(n2_t[:], n2)
         nc.sync.dma_start(gn_t[:], gn.rearrange("(p t) o -> p (t o)", t=PACK))
-        nc.sync.dma_start(w23_raw[:, 0], w2.rearrange("(p j) c -> p j c", j=PACK))
-        nc.sync.dma_start(w23_raw[:, 1], w3.rearrange("(p j) c -> p j c", j=PACK))
+        nc.sync.dma_start(w2_raw, w2.rearrange("(p j) c -> p j c", j=PACK))
+        nc.sync.dma_start(w3_raw, w3.rearrange("(p j) c -> p j c", j=PACK))
         nc.sync.dma_start(n4_t[:], n4)
         with nc.allow_non_contiguous_dma(reason="one rate for each partition and row tile"):
             nc.sync.dma_start(tau_t[:], tau.rearrange("(m p) o -> p (m o)", p=P))
 
         w1_bf = held("w1_bf", [P, PACK, P, PACK], BF16)
         w1_dst = w1_bf[:].rearrange("p t m j -> p m j t")
-        w1_src = w1_raw[:].rearrange("p j (m t) -> p m j t", t=PACK)
+        w1_src = w1_raw.rearrange("p j (m t) -> p m j t", t=PACK)
         nc.scalar.activation(w1_dst[:, : P // 2], w1_src[:, : P // 2], ACT.Copy)
         nc.vector.tensor_copy(w1_dst[:, P // 2 :], w1_src[:, P // 2 :])
         x_bytes = held("x_bytes", [P, S], U8)
@@ -110,16 +113,14 @@ def tile_picked_mixhoddsegl_none_p_kernel(
         )
         x_codes = held("x_codes", [P, S], U32)
 
-        ex = held("ex", [P, PACK, S], F32)
-        for a in range(0, S, HALF):
-            cols = slice(a, a + HALF)
-            nc.vector.tensor_copy(x_codes[:, cols], xw[:].indirect(entries(offs_t, a, a + HALF)))
-            for pair in range(2):
-                y_bank = psum.tile([P, 2, HALF], F32, name="y%d_%d" % (a, pair))
-                for u in range(2):
-                    rows = slice((2 * pair + u) * P, (2 * pair + u + 1) * P)
-                    mx(y_bank[:, u, :], w1_codes[:, rows], w1_scales[:, rows], x_codes[:, cols], x_bytes[:, cols], True, True)
-                nc.scalar.activation(ex[:, 2 * pair : 2 * pair + 2, cols], y_bank[:], ACT.Exp, scale=0.5)
+        for a in range(0, S, CHUNK):
+            cols = slice(a, a + CHUNK)
+            nc.vector.tensor_copy(x_codes[:, cols], xw[:].indirect(entries(offs_t, a, a + CHUNK)))
+            y_bank = psum.tile([P, PACK, CHUNK], F32, name="y%d" % a)
+            for t in range(PACK):
+                rows = slice(t * P, (t + 1) * P)
+                mx(y_bank[:, t, :], w1_codes[:, rows], w1_scales[:, rows], x_codes[:, cols], x_bytes[:, cols], True, True)
+            nc.scalar.activation(ex[:, :PACK, cols], y_bank[:], ACT.Exp, scale=0.5)
 
         hz_codes = held("hz_codes", [P, S], U32)
         hz_bytes = held("hz_bytes", [P, S], U8)
@@ -131,10 +132,8 @@ def tile_picked_mixhoddsegl_none_p_kernel(
                     hz_scales[2 * odd + e : P : 32, :].bitcast(I32), hz_bytes[LANES * odd + e : P : 32, :].bitcast(I32)
                 )
 
-        ex_n2 = held("ex_n2", [P, PACK, S], F32)
         for t in range(PACK):
-            for a in range(0, S, HALF):
-                nc.vector.tensor_copy(ex_n2[:, t, a : a + HALF], ex[:, t, :].indirect(entries(n2_t, a, a + HALF)))
+            nc.vector.tensor_copy(ex_n2[:, t, :], ex_window(t).indirect(n2_t[:]))
 
         w23_codes = [held("w23_codes%d" % m, [P, 2 * P], U32) for m in range(4)]
         w23_scales = [held("w23_scales%d" % m, [P, 2 * P], U8) for m in range(4)]
@@ -144,10 +143,11 @@ def tile_picked_mixhoddsegl_none_p_kernel(
 
         def quantize_w23(m):
             bf = stage("w23_bf", [P, 2, P, PACK], BF16)
-            nc.vector.tensor_copy(
-                bf[:].rearrange("p w (c i) j -> p w c j i", i=4),
-                w23_raw[:, :, :, m * P : (m + 1) * P].rearrange("p w j (c i) -> p w c j i", i=4),
-            )
+            for w, raw in enumerate((w2_raw, w3_raw)):
+                nc.vector.tensor_copy(
+                    bf[:, w].rearrange("p (c i) j -> p c j i", i=4),
+                    raw[:, :, m * P : (m + 1) * P].rearrange("p j (c i) -> p c j i", i=4),
+                )
             nc.vector.quantize_mx(
                 out=w23_codes[m][:].bitcast(FP8X4),
                 scales=w23_scales[m][:],
@@ -157,42 +157,45 @@ def tile_picked_mixhoddsegl_none_p_kernel(
         z_codes = held("z_codes", [P, S], U32)
         z_scales = held("z_scales", [P, S], U8)
         h_bank = [psum.tile([P, S], F32, name="hb%d" % m) for m in range(4)]
-        h_end = psum.tile([P, CHUNK], F32, name="h_end", tag="y0_0")
+        h_end = psum.tile([P, S // 2], F32, name="h_end", tag="y0")
         bias = held("bias", [P, 4], F32)
-        sums = {}
+        last = S - CHUNK
+        half = S // 2
+        fetched_first = held("fetched_first", [P, 2, PACK, FIRST], F32)
+        sums_first = keep.tile([P, 2, PACK, FIRST], F32, name="sums_first", tag="turn")
+        sums_last = held("sums_last", [P, 2, PACK, S - FIRST], F32)
+        logs = held("logs", [P, 2, PACK, S], F32)
+        diff = held("diff", [P, PACK, S], F32)
+        z_bf = held("z_bf", [P, S, PACK], BF16)
 
-        def look_up(a):
-            b = a + CHUNK
-            ab = pair_ring.tile([P, 2, PACK, CHUNK], F32, name="ab")
-            ex_n3 = pair_ring.tile([P, PACK, CHUNK], F32, name="ex_n3")
-            for t in range(PACK):
-                nc.scalar.activation(ex_n3[:, t, :], ex[:, t, :].indirect(entries(n3_t, a, b)), ACT.Copy)
-            for t in range(PACK):
-                nc.scalar.activation(ab[:, 0, t, :], ex[:, t, :].indirect(entries(n1_t, a, b)), ACT.Copy)
-            nc.vector.tensor_tensor(ab[:, 1], ex_n2[:, :, a:b], ex_n3[:], ALU.add)
-            nc.vector.tensor_tensor(ab[:, 0], ab[:, 0], ex[:, :, a:b], ALU.add)
-            sums[a] = ab
+        def look_up(a, b, fetched, sums, rows_per_add):
+            for which, list_tile in ((1, n3_t), (0, n1_t)):
+                other = ex_n2 if which else ex
+                for t in range(PACK):
+                    nc.scalar.activation(fetched[:, which, t, :], ex_window(t).indirect(entries(list_tile, a, b)), ACT.Copy)
+                    if (t + 1) % rows_per_add == 0:
+                        rows = slice(t + 1 - rows_per_add, t + 1)
+                        nc.vector.tensor_tensor(
+                            sums[:, which, rows, :], fetched[:, which, rows, :], other[:, rows, a:b], ALU.add
+                        )
 
-        def make_z(a, parts):
-            b = a + CHUNK
-            ab = sums[a]
-            logs = pair_ring.tile([P, 2, PACK, CHUNK], F32, name="logs")
-            diff = pair_ring.tile([P, PACK, CHUNK], F32, name="diff")
-            z_bf = pair_ring.tile([P, CHUNK, PACK], BF16, name="z_bf", align_bytes=64)
-            step = CHUNK // parts
-            for c in range(0, CHUNK, step):
-                cols = slice(c, c + step)
-                nc.scalar.activation(logs[:, :, :, cols], ab[:, :, :, cols], ACT.Ln)
-                nc.vector.tensor_tensor(diff[:, :, cols], logs[:, 0, :, cols], logs[:, 1, :, cols], ALU.subtract)
-                nc.vector.tensor_tensor(
-                    z_bf[:, cols, :].rearrange("p (c i) t -> p c t i", i=4),
-                    diff[:, :, cols].rearrange("p t (c i) -> p c t i", i=4),
-                    gn_t[:].unsqueeze(1).unsqueeze(3).to_broadcast([P, step // 4, PACK, 4]),
-                    ALU.mult,
-                )
-            nc.vector.quantize_mx(
-                out=z_codes[:, a:b].bitcast(FP8X4), scales=z_scales[:, a:b], in_=z_bf[:].rearrange("p n t -> p (n t)")
+        def make_z(sums, base, a, b):
+            nc.scalar.activation(logs[:, :, :, a:b], sums[:, :, :, a - base : b - base], ACT.Ln)
+            nc.vector.tensor_tensor(diff[:, :, a:b], logs[:, 0, :, a:b], logs[:, 1, :, a:b], ALU.subtract)
+            nc.vector.tensor_tensor(
+                z_bf[:, a:b, :].rearrange("p (c i) t -> p c t i", i=4),
+                diff[:, :, a:b].rearrange("p t (c i) -> p c t i", i=4),
+                gn_t[:].unsqueeze(1).unsqueeze(3).to_broadcast([P, (b - a) // 4, PACK, 4]),
+                ALU.mult,
             )
+            if b % CHUNK == 0:
+                cols = slice(b - CHUNK, b)
+                nc.vector.quantize_mx(
+                    out=z_codes[:, cols].bitcast(FP8X4),
+                    scales=z_scales[:, cols],
+                    in_=z_bf[:, cols, :].rearrange("p n t -> p (n t)"),
+                )
+                product(h_bank[0][:, cols] if b <= half else h_end[:, b - CHUNK - half : b - half], 0, b - CHUNK, b)
 
         def product(dst, m, a, b):
             mx(dst, w23_codes[m][:, P:], w23_scales[m][:, P:], hz_codes[:, a:b], hz_scales[:, a:b], True, False)
@@ -204,20 +207,20 @@ def tile_picked_mixhoddsegl_none_p_kernel(
         def make_bias(m, top):
             nc.vector.tensor_scalar(bias[:, m : m + 1], top, tau_t[:, m : m + 1], -1.0, ALU.mult, ALU.mult)
 
-        last = S - CHUNK
-        look_up(0)
+        look_up(0, FIRST, fetched_first, sums_first, 2)
         quantize_w23(0)
-        for a in range(0, last, CHUNK):
-            look_up(a + CHUNK)
-            make_z(a, 1)
-            product(h_bank[0][:, a : a + CHUNK], 0, a, a + CHUNK)
+        for a in range(0, FIRST, CHUNK):
+            make_z(sums_first, 0, a, min(a + CHUNK, FIRST))
         tops = stage("tops", [P, 2], F32)
-        evacuate(h_t[0][:, :last], h_bank[0][:, :last], None, tops[:, 0:1])
-        make_z(last, 2)
-        product(h_end[:], 0, last, S)
-        evacuate(h_t[0][:, last:S], h_end[:], tops[:, 0:1], tops[:, 1:2])
+        evacuate(h_t[0][:, :half], h_bank[0][:, :half], None, tops[:, 0:1])
+        fetched_last = keep.tile([P, 2, PACK, S - FIRST], F32, name="fetched_last", tag="turn")
+        look_up(FIRST, S, fetched_last, sums_last, 1)
+        for a, b in ((320, 384), (384, 448), (448, 480), (480, 512)):
+            make_z(sums_last, FIRST, a, b)
+        evacuate(h_t[0][:, half:S], h_end[:], tops[:, 0:1], tops[:, 1:2])
         make_bias(0, tops[:, 1:2])
 
+        later_tops = held("later_tops", [P, 4], F32)
         ms = held("ms", [P, 4, S], F32)
 
         def members(m):
@@ -237,22 +240,19 @@ def tile_picked_mixhoddsegl_none_p_kernel(
                     ALU.add,
                 )
 
+        for m in range(1, 4):
+            quantize_w23(m)
+            product(h_bank[m][:], m, 0, S)
+            evacuate(h_t[m][:, :S], h_bank[m][:], None, later_tops[:, m : m + 1])
+            make_bias(m, later_tops[:, m : m + 1])
         for m in range(4):
-            if m + 1 < 4:
-                quantize_w23(m + 1)
-                product(h_bank[m + 1][:], m + 1, 0, S)
-                top = stage("top", [P, 1], F32)
-                evacuate(h_t[m + 1][:, :S], h_bank[m + 1][:], None, top[:])
-                make_bias(m + 1, top[:])
             members(m)
 
         last_log = held("last_log", [P, S], F32)
         result = held("result", [P, 4, S], F32)
         for m in range(4):
             log_ms = last_log[:] if m == 3 else h_t[3][:, (m + 1) * S : (m + 2) * S]
-            step = S // 2 if m == 3 else S
-            for a in range(0, S, step):
-                cols = slice(a, a + step)
+            for cols in (slice(0, half), slice(half, last), slice(last, S)) if m == 3 else (slice(0, half), slice(half, S)):
                 nc.scalar.activation(log_ms[:, cols], ms[:, m, cols], ACT.Ln, bias=0.25)
                 nc.vector.scalar_tensor_tensor(
                     result[:, m, cols], h_t[m][:, cols], -0.5, log_ms[:, cols], ALU.mult, ALU.add

@@ -81,10 +81,12 @@ def tile_picked_mixhoddsegl_none_p_kernel(
         nc.vector.memset(hz_scales[:].bitcast(I32), 0)
         nc.vector.memset(ex[:, PACK, :], 0.0)
 
-        nc.sync.dma_start(w1_raw, w1.rearrange("(p j) c -> p j c", j=PACK))
+        w1_rows = w1.rearrange("(p j) c -> p j c", j=PACK)
+        nc.sync.dma_start(w1_raw[:, :2, :], w1_rows[:, :2, :])
         for q in range(4):
             nc.sync.dma_start(xs[32 * q : 32 * q + 4, :].bitcast(I32), scale_rows[4 * q : 4 * q + 4, :])
         nc.sync.dma_start(offs_t[:], offs)
+        nc.sync.dma_start(w1_raw[:, 2:, :], w1_rows[:, 2:, :])
         nc.sync.dma_start(xw[:].bitcast(I32), x_words[0].rearrange("p n t -> p (n t)").bitcast(I32))
         nc.sync.dma_start(hz_t[:], hz)
         for e in range(2):
@@ -99,13 +101,14 @@ def tile_picked_mixhoddsegl_none_p_kernel(
         with nc.allow_non_contiguous_dma(reason="one rate for each partition and row tile"):
             nc.sync.dma_start(tau_t[:], tau.rearrange("(m p) o -> p (m o)", p=P))
 
+        x_bytes = held("x_bytes", [P, S], U8)
+        nc.vector.tensor_copy(x_bytes[:], xs[:].indirect(offs_t[:]))
+
         w1_bf = held("w1_bf", [P, PACK, P, PACK], BF16)
         w1_dst = w1_bf[:].rearrange("p t m j -> p m j t")
         w1_src = w1_raw.rearrange("p j (m t) -> p m j t", t=PACK)
         nc.scalar.activation(w1_dst[:, : P // 2], w1_src[:, : P // 2], ACT.Copy)
         nc.vector.tensor_copy(w1_dst[:, P // 2 :], w1_src[:, P // 2 :])
-        x_bytes = held("x_bytes", [P, S], U8)
-        nc.vector.tensor_copy(x_bytes[:], xs[:].indirect(offs_t[:]))
         w1_codes = held("w1_codes", [P, H], U32)
         w1_scales = held("w1_scales", [P, H], U8)
         nc.vector.quantize_mx(

@@ -107,8 +107,7 @@ def tile_picked_mixhoddsegl_none_p_kernel(
         w1_bf = held("w1_bf", [P, PACK, P, PACK], BF16)
         w1_dst = w1_bf[:].rearrange("p t m j -> p m j t")
         w1_src = w1_raw.rearrange("p j (m t) -> p m j t", t=PACK)
-        nc.scalar.activation(w1_dst[:, : P // 2], w1_src[:, : P // 2], ACT.Copy)
-        nc.vector.tensor_copy(w1_dst[:, P // 2 :], w1_src[:, P // 2 :])
+        nc.vector.tensor_copy(w1_dst, w1_src)
         w1_codes = held("w1_codes", [P, H], U32)
         w1_scales = held("w1_scales", [P, H], U8)
         nc.vector.quantize_mx(

@@ -107,7 +107,8 @@ def tile_picked_mixhoddsegl_none_p_kernel(
         w1_bf = held("w1_bf", [P, PACK, P, PACK], BF16)
         w1_dst = w1_bf[:].rearrange("p t m j -> p m j t")
         w1_src = w1_raw.rearrange("p j (m t) -> p m j t", t=PACK)
-        nc.vector.tensor_copy(w1_dst, w1_src)
+        nc.scalar.activation(w1_dst[:, :, :2, :], w1_src[:, :, :2, :], ACT.Copy)
+        nc.vector.tensor_copy(w1_dst[:, :, 2:, :], w1_src[:, :, 2:, :])
         w1_codes = held("w1_codes", [P, H], U32)
         w1_scales = held("w1_scales", [P, H], U8)
         nc.vector.quantize_mx(

from contextlib import ExitStack

import concourse.mybir as mybir

K, T, S, N, H, W = 512, 2048, 512, 512, 512, 2048
FLOPS = 3 * 2 * 512 * 512 * 512

F32 = mybir.dt.float32
BF16 = mybir.dt.bfloat16
I32 = mybir.dt.int32
U32 = mybir.dt.uint32
U16 = mybir.dt.uint16
U8 = mybir.dt.uint8
FP8X4 = mybir.dt.float8_e4m3fn_x4
ACT = mybir.ActivationFunctionType
ALU = mybir.AluOpType
AX = mybir.AxisListType

P = 128
PACK = 4
LANES = 16
CHUNK = 128
PIECE = 1024
FIRST = 320
SHORT = 64
MEMBERS = 4


def tile_picked_mixhoddsegl_none_p_kernel(
    tc, x_words, x_scales, w1, gn, w2, w3, tau, offs, n1, n2, n3, hz, n4, out
):
    nc = tc.nc

    def entries(list_tile, a, b):
        return list_tile[:, a // LANES : b // LANES]

    def mx(dst, lhs_codes, lhs_scales, rhs_codes, rhs_scales, start, stop):
        nc.tensor.matmul_mx(
            out=dst,
            lhsT=lhs_codes.bitcast(FP8X4),
            lhsT_scale=lhs_scales,
            rhs=rhs_codes.bitcast(FP8X4),
            rhs_scale=rhs_scales,
            start=start,
            stop=stop,
        )

    with ExitStack() as ctx:
        keep = ctx.enter_context(tc.tile_pool(name="keep", bufs=1))
        ring = ctx.enter_context(tc.tile_pool(name="ring", bufs=6))
        psum = ctx.enter_context(tc.psum_pool(name="psum", bufs=1))

        def held(name, shape, dtype):
            return keep.tile(shape, dtype, name=name, align_bytes=64)

        offs_t = held("offs_t", [P, S // LANES], U16)
        n1_t = held("n1_t", [P, S // LANES], U16)
        n2_t = held("n2_t", [P, S // LANES], U16)
        n3_t = held("n3_t", [P, S // LANES], U16)
        hz_t = held("hz_t", [P, S // LANES], U16)
        n4_t = held("n4_t", [P, W // LANES], U16)

        xw = held("xw", [P, T], U32)
        xs = held("xs", [P, T], U8)
        hs = held("hs", [P, T], U8)
        gn_t = held("gn_t", [P, PACK], F32)
        tau_t = held("tau_t", [P, PACK], F32)
        hz_scales = held("hz_scales", [P, S], U8)
        h_t = [held("h%d" % m, [P, (1 + PACK) * S], F32) for m in range(4)]
        ex_n2, w1_raw, w2_raw, w3_raw = [h[:, S:].rearrange("p (j c) -> p j c", j=PACK) for h in h_t]
        ex = held("ex", [P, PACK + 1, S], F32)
        ex_row = ex[:].rearrange("p t s -> p (t s)")

        def ex_window(t):
            return ex_row[:, t * S : (t + 2) * S]

        scale_rows = x_scales[0].bitcast(I32)

        nc.vector.memset(xs[:].bitcast(I32), 0)
        nc.vector.memset(hs[:].bitcast(I32), 0)
        nc.vector.memset(hz_scales[:].bitcast(I32), 0)
        nc.vector.memset(ex[:, PACK, :], 0.0)

        w1_rows = w1.rearrange("(p j) c -> p j c", j=PACK)
        nc.sync.dma_start(w1_raw[:, :2, :], w1_rows[:, :2, :])
        for q in range(4):
            nc.sync.dma_start(xs[32 * q : 32 * q + 4, :].bitcast(I32), scale_rows[4 * q : 4 * q + 4, :])
        nc.sync.dma_start(offs_t[:], offs)
        nc.sync.dma_start(w1_raw[:, 2:, :], w1_rows[:, 2:, :])
        nc.sync.dma_start(xw[:].bitcast(I32), x_words[0].rearrange("p n t -> p (n t)").bitcast(I32))
        nc.sync.dma_start(hz_t[:], hz)
        for e in range(2):
            nc.sync.dma_start(hs[e:P:LANES, :].bitcast(I32), scale_rows[e:16:2, :])
        nc.sync.dma_start(n3_t[:], n3)
        nc.sync.dma_start(n1_t[:], n1)
        nc.sync.dma_start(n2_t[:], n2)
        nc.sync.dma_start(gn_t[:], gn.rearrange("(p t) o -> p (t o)", t=PACK))
        nc.sync.dma_start(w2_raw, w2.rearrange("(p j) c -> p j c", j=PACK))
        nc.sync.dma_start(w3_raw, w3.rearrange("(p j) c -> p j c", j=PACK))
        nc.sync.dma_start(n4_t[:], n4)
        with nc.allow_non_contiguous_dma(reason="one rate for each partition and row tile"):
            nc.sync.dma_start(tau_t[:], tau.rearrange("(m p) o -> p (m o)", p=P))

        x_bytes = held("x_bytes", [P, S], U8)
        nc.vector.tensor_copy(x_bytes[:], xs[:].indirect(offs_t[:]))

        w1_bf = held("w1_bf", [P, PACK, P, PACK], BF16)
        w1_dst = w1_bf[:].rearrange("p t m j -> p m j t")
        w1_src = w1_raw.rearrange("p j (m t) -> p m j t", t=PACK)
        nc.scalar.activation(w1_dst[:, :, :2, :], w1_src[:, :, :2, :], ACT.Copy)
        nc.vector.tensor_copy(w1_dst[:, :, 2:, :], w1_src[:, :, 2:, :])
        w1_codes = held("w1_codes", [P, H], U32)
        w1_scales = held("w1_scales", [P, H], U8)
        nc.vector.quantize_mx(
            out=w1_codes[:].bitcast(FP8X4), scales=w1_scales[:], in_=w1_bf[:].rearrange("p t m j -> p (t m j)")
        )
        x_codes = held("x_codes", [P, S], U32)

        for a in range(0, S, CHUNK):
            cols = slice(a, a + CHUNK)
            nc.vector.tensor_copy(x_codes[:, cols], xw[:].indirect(entries(offs_t, a, a + CHUNK)))
            y_bank = psum.tile([P, PACK, CHUNK], F32, name="y%d" % a)
            for t in range(PACK):
                rows = slice(t * P, (t + 1) * P)
                mx(y_bank[:, t, :], w1_codes[:, rows], w1_scales[:, rows], x_codes[:, cols], x_bytes[:, cols], True, True)
            nc.scalar.activation(ex[:, :PACK, cols], y_bank[:], ACT.Exp, scale=0.5)

        hz_codes = held("hz_codes", [P, S], U32)
        hz_bytes = held("hz_bytes", [P, S], U8)
        nc.vector.tensor_copy(hz_codes[:], xw[:].indirect(hz_t[:]))
        nc.vector.tensor_copy(hz_bytes[:], hs[:].indirect(hz_t[:]))
        for odd in range(2):
            for e in range(2):
                nc.sync.dma_start(
                    hz_scales[2 * odd + e : P : 32, :].bitcast(I32), hz_bytes[LANES * odd + e : P : 32, :].bitcast(I32)
                )

        for t in range(PACK):
            nc.vector.tensor_copy(ex_n2[:, t, :], ex_window(t).indirect(n2_t[:]))

        w23_codes = [held("w23_codes%d" % m, [P, 2 * P], U32) for m in range(4)]
        w23_scales = [held("w23_scales%d" % m, [P, 2 * P], U8) for m in range(4)]

        def stage(name, shape, dtype):
            return keep.tile(shape, dtype, name=name, tag="stage", align_bytes=64)

        def quantize_w23(m):
            bf = stage("w23_bf", [P, 2, P, PACK], BF16)
            for w, raw in enumerate((w2_raw, w3_raw)):
                nc.vector.tensor_copy(
                    bf[:, w].rearrange("p (c i) j -> p c j i", i=4),
                    raw[:, :, m * P : (m + 1) * P].rearrange("p j (c i) -> p c j i", i=4),
                )
            nc.vector.quantize_mx(
                out=w23_codes[m][:].bitcast(FP8X4),
                scales=w23_scales[m][:],
                in_=bf[:].rearrange("p w c j -> p (w c j)"),
            )

        z_codes = held("z_codes", [P, S], U32)
        z_scales = held("z_scales", [P, S], U8)
        h_bank = [psum.tile([P, S], F32, name="hb%d" % m) for m in range(4)]
        h_end = psum.tile([P, S // 2], F32, name="h_end", tag="y0")
        bias = held("bias", [P, 4], F32)
        last = S - CHUNK
        half = S // 2
        fetched_first = held("fetched_first", [P, 2, PACK, FIRST], F32)
        sums_first = keep.tile([P, 2, PACK, FIRST], F32, name="sums_first", tag="turn")
        sums_last = held("sums_last", [P, 2, PACK, S - FIRST], F32)
        logs = held("logs", [P, 2, PACK, S], F32)
        diff = held("diff", [P, PACK, S], F32)
        z_bf = held("z_bf", [P, S, PACK], BF16)

        def look_up(a, b, fetched, sums, rows_per_add):
            for which, list_tile in ((1, n3_t), (0, n1_t)):
                other = ex_n2 if which else ex
                for t in range(PACK):
                    nc.scalar.activation(fetched[:, which, t, :], ex_window(t).indirect(entries(list_tile, a, b)), ACT.Copy)
                    if (t + 1) % rows_per_add == 0:
                        rows = slice(t + 1 - rows_per_add, t + 1)
                        nc.vector.tensor_tensor(
                            sums[:, which, rows, :], fetched[:, which, rows, :], other[:, rows, a:b], ALU.add
                        )

        def make_z(sums, base, a, b):
            nc.scalar.activation(logs[:, :, :, a:b], sums[:, :, :, a - base : b - base], ACT.Ln)
            nc.vector.tensor_tensor(diff[:, :, a:b], logs[:, 0, :, a:b], logs[:, 1, :, a:b], ALU.subtract)
            nc.vector.tensor_tensor(
                z_bf[:, a:b, :].rearrange("p (c i) t -> p c t i", i=4),
                diff[:, :, a:b].rearrange("p t (c i) -> p c t i", i=4),
                gn_t[:].unsqueeze(1).unsqueeze(3).to_broadcast([P, (b - a) // 4, PACK, 4]),
                ALU.mult,
            )
            if b % CHUNK == 0:
                cols = slice(b - CHUNK, b)
                nc.vector.quantize_mx(
                    out=z_codes[:, cols].bitcast(FP8X4),
                    scales=z_scales[:, cols],
                    in_=z_bf[:, cols, :].rearrange("p n t -> p (n t)"),
                )
                product(h_bank[0][:, cols] if b <= half else h_end[:, b - CHUNK - half : b - half], 0, b - CHUNK, b)

        def product(dst, m, a, b):
            mx(dst, w23_codes[m][:, P:], w23_scales[m][:, P:], hz_codes[:, a:b], hz_scales[:, a:b], True, False)
            mx(dst, w23_codes[m][:, :P], w23_scales[m][:, :P], z_codes[:, a:b], z_scales[:, a:b], False, True)

        def evacuate(dst, src, so_far, top):
            nc.vector.tensor_scalar(dst, src, 1.0, so_far, ALU.mult, ALU.max, accum_out=top)

        def make_bias(m, top):
            nc.vector.tensor_scalar(bias[:, m : m + 1], top, tau_t[:, m : m + 1], -1.0, ALU.mult, ALU.mult)

        look_up(0, FIRST, fetched_first, sums_first, 2)
        quantize_w23(0)
        for a in range(0, FIRST, CHUNK):
            make_z(sums_first, 0, a, min(a + CHUNK, FIRST))
        tops = stage("tops", [P, 2], F32)
        evacuate(h_t[0][:, :half], h_bank[0][:, :half], None, tops[:, 0:1])
        fetched_last = keep.tile([P, 2, PACK, S - FIRST], F32, name="fetched_last", tag="turn")
        look_up(FIRST, S, fetched_last, sums_last, 1)
        for a, b in ((320, 384), (384, 448), (448, 480), (480, 512)):
            make_z(sums_last, FIRST, a, b)
        evacuate(h_t[0][:, half:S], h_end[:], tops[:, 0:1], tops[:, 1:2])
        make_bias(0, tops[:, 1:2])

        later_tops = held("later_tops", [P, 4], F32)
        ms = held("ms", [P, 4, S], F32)

        def members(m):
            for a in range(0, W, PIECE):
                ea = ring.tile([P, PIECE], F32, name="ea")
                nc.scalar.activation(
                    ea[:],
                    h_t[m][:].indirect(entries(n4_t, a, a + PIECE)),
                    ACT.Exp,
                    bias=bias[:, m : m + 1],
                    scale=tau_t[:, m : m + 1],
                )
                nc.vector.tensor_reduce(
                    ms[:, m, a // MEMBERS : (a + PIECE) // MEMBERS],
                    ea[:].rearrange("p (j t) -> p j t", t=MEMBERS),
                    AX.X,
                    ALU.add,
                )

        for m in range(1, 4):
            quantize_w23(m)
            product(h_bank[m][:], m, 0, S)
            evacuate(h_t[m][:, :S], h_bank[m][:], None, later_tops[:, m : m + 1])
            make_bias(m, later_tops[:, m : m + 1])
        for m in range(4):
            members(m)

        last_log = held("last_log", [P, S], F32)
        result = held("result", [P, 4, S], F32)
        for m in range(4):
            log_ms = last_log[:] if m == 3 else h_t[3][:, (m + 1) * S : (m + 2) * S]
            for cols in (slice(0, half), slice(half, last), slice(last, S)) if m == 3 else (slice(0, half), slice(half, S)):
                nc.scalar.activation(log_ms[:, cols], ms[:, m, cols], ACT.Ln, bias=0.25)
                nc.vector.scalar_tensor_tensor(
                    result[:, m, cols], h_t[m][:, cols], -0.5, log_ms[:, cols], ALU.mult, ALU.add
                )
                nc.sync.dma_start(out[m * P : (m + 1) * P, cols], result[:, m, cols])
